import numpy as np
import ml_dtypes


def mxq(x, axis, fmt="e4m3"):
    dtype, down = {"e4m3": (ml_dtypes.float8_e4m3fn, 7), "e5m2": (ml_dtypes.float8_e5m2, 14)}[fmt]
    v = np.moveaxis(np.asarray(x, np.float32).astype(ml_dtypes.bfloat16).astype(np.float64), axis, -1)
    blocks = v.reshape(v.shape[:-1] + (-1, 32))
    amax = np.abs(blocks).max(-1, keepdims=True)
    byte = np.maximum(np.where(amax > 0, np.frexp(amax)[1] - 1 + 127, 0) - down, 1)
    scale = np.exp2(byte - 127.0)
    codes = (blocks / scale).astype(np.float32).astype(dtype).astype(np.float64)
    return np.moveaxis((codes * scale).reshape(v.shape), -1, axis)


WIDE = False


def mx_kscale(k):
    if not WIDE:
        return np.ones(k)
    levels = np.array([30, -30])
    if k % 512:
        return np.exp2(np.random.permutation(np.resize(levels, k // 32))).repeat(32)
    a = np.empty((k // 512, 16))
    for p in range(k // 512):
        a[p, :8] = np.random.permutation(np.resize(levels, 8))
        for g in range(8):
            far = levels[np.abs(levels - a[p, g]) >= 10]
            a[p, g + 8] = far[np.random.randint(len(far))]
    return np.exp2(a.ravel()).repeat(32)


def f64(x):
    return np.asarray(x).astype(np.float64)


def striped(idx):
    return np.tile(idx.reshape(-1, 16).T, (8, 1)).astype(np.uint16)


def unstriped(offs):
    return offs[:16].T.reshape(-1).astype(np.int64)


K, T, E, C, N = 256, 2560, 2, 1024, 512


def setup_inputs():
    n = np.random.standard_normal
    idx = np.random.permutation(T)[:E * C]
    s = mx_kscale(E * C)[None, :]
    xT = n((K, T)); dyT = n((N, T))
    xT[:, idx] *= s; dyT[:, idx] /= s
    return {
        "xT": xT.astype(np.float32),
        "dyT": dyT.astype(np.float32),
        "gate": np.tile(np.random.uniform(0.2, 1.0, E * C), (N, 1)).astype(np.float32),
        "offs": striped(idx),
    }


def reference(xT, dyT, gate, offs):
    idx = unstriped(offs)
    xq = mxq(f64(xT)[:, idx], 1, "e4m3")
    gq = mxq(f64(gate) * f64(dyT)[:, idx], 1, "e5m2")
    return np.stack([(xq[:, e * C:(e + 1) * C] @ gq[:, e * C:(e + 1) * C].T) for e in range(E)])

@@ -1,0 +1,169 @@
+from contextlib import ExitStack
+
+import concourse.mybir as mybir
+from concourse.masks import make_identity
+
+K, T, E, C, N = 256, 2560, 2, 1024, 512
+S = E * C
+
+FLOPS = 2 * S * K * N
+BYTES = 4 * (K * T + N * T + S + E * K * N) + 2 * S
+
+F32 = mybir.dt.float32
+BF16 = mybir.dt.bfloat16
+U32 = mybir.dt.uint32
+U16 = mybir.dt.uint16
+U8 = mybir.dt.uint8
+E4M3X4 = mybir.dt.float8_e4m3fn_x4
+E5M2X4 = mybir.dt.float8_e5m2_x4
+MULT = mybir.AluOpType.mult
+
+P = 128
+PACK = 4
+PASS = P * PACK
+PASSES = S // PASS
+XB = K // P
+GB = N // P
+X_CHUNK = 640
+
+
+def tile_moe_bdw_lin_none_kernel(tc, xT, dyT, gate, offs, out):
+    nc = tc.nc
+    with ExitStack() as ctx:
+        keep = ctx.enter_context(tc.tile_pool(name="keep", bufs=1))
+        work = ctx.enter_context(tc.tile_pool(name="work", bufs=3))
+        psum = ctx.enter_context(tc.psum_pool(name="psum", bufs=4))
+        acc_pool = ctx.enter_context(tc.psum_pool(name="acc_pool", bufs=4))
+
+        offsets = keep.tile([P, S // 16], U16, name="offsets")
+        nc.sync.dma_start(offsets[:], offs)
+        gate_rows = keep.tile([P, P], F32, name="gate_rows")
+        nc.sync.dma_start(gate_rows[:], gate[0 : P * P // S, :].rearrange("r (c p) -> (r c) p", p=P))
+
+        dy = [keep.tile([P, T], F32, name=f"dy{b}") for b in range(GB)]
+        x_raw = [keep.tile([P, XB, X_CHUNK], F32, name=f"xraw{i}") for i in range(T // X_CHUNK)]
+        for b in range(GB - 1):
+            nc.sync.dma_start(dy[b][:], dyT[b * P : (b + 1) * P, :])
+        for i in range(T // X_CHUNK):
+            nc.sync.dma_start(x_raw[i][:], xT[:, i * X_CHUNK : (i + 1) * X_CHUNK].rearrange("(h p) t -> p h t", p=P))
+        nc.sync.dma_start(dy[GB - 1][:], dyT[(GB - 1) * P : GB * P, :])
+
+        ident_f = keep.tile([P, P], F32, name="ident_f")
+        make_identity(nc, ident_f[:])
+        ident_b = keep.tile([P, P], BF16, name="ident_b")
+        make_identity(nc, ident_b[:])
+
+        gate_bank = psum.tile([P, P], F32, name="bank")
+        nc.tensor.transpose(gate_bank[:], gate_rows[:], ident_f[:])
+        gate_cols = keep.tile([P, S // P], F32, name="gate_cols")
+        nc.scalar.copy(gate_cols[:], gate_bank[:, 0 : S // P])
+        gates = keep.tile([P, S], F32, name="gates")
+        for c in range(PASSES):
+            bank = psum.tile([P, PACK, P], F32, name="bank")
+            for t in range(PACK):
+                col = PACK * c + t
+                nc.tensor.transpose(bank[:, t, :], gate_cols[:, col : col + 1].to_broadcast([P, P]), ident_f[:])
+            nc.scalar.copy(gates[:, c * PASS : (c + 1) * PASS], bank[:].rearrange("p t n -> p (t n)"))
+
+        xp = keep.tile([P, T, XB], BF16, name="xp", align_bytes=64)
+
+        g_turned = [keep.tile([P, N, PACK], BF16, name=f"gt{c}", align_bytes=64) for c in range(PASSES)]
+        g_codes = [keep.tile([P, N], U32, name=f"gc{c}", align_bytes=64) for c in range(PASSES)]
+        g_scales = [keep.tile([P, N], U8, name=f"gs{c}", align_bytes=64) for c in range(PASSES)]
+        x_turned = [keep.tile([P, 2, K, PACK], BF16, name=f"xt{i}", align_bytes=64) for i in range(PASSES // 2)]
+        x_codes = [keep.tile([P, 2, K], U32, name=f"xc{i}", align_bytes=64) for i in range(PASSES // 2)]
+        x_scales = [keep.tile([P, 2, K], U8, name=f"xs{i}", align_bytes=64) for i in range(PASSES // 2)]
+
+        def gather_g(b, lo, hi):
+            g = work.tile([P, hi - lo], F32, name=f"g{hi - lo}")
+            nc.vector.tensor_tensor(g[:], dy[b][:].indirect(offsets[:, lo // 16 : hi // 16]), gates[:, lo:hi], MULT)
+            for c in range(lo // PASS, hi // PASS):
+                bank = psum.tile([P, PACK, P], F32, name="bank")
+                quads = g[:, c * PASS - lo : (c + 1) * PASS - lo].rearrange("p (q t) -> p q t", t=PACK)
+                for t in range(PACK):
+                    nc.tensor.transpose(bank[:, t, :], quads[:, :, t], ident_f[:])
+                nc.scalar.copy(g_turned[c][:, b * P : (b + 1) * P, :], bank[:].rearrange("p t n -> p n t"))
+
+        def quantize_g(c, b0, b1):
+            cols = slice(b0 * P, b1 * P)
+            nc.vector.quantize_mx(
+                out=g_codes[c][:, cols].bitcast(E5M2X4),
+                scales=g_scales[c][:, cols],
+                in_=g_turned[c][:, cols, :].rearrange("p n t -> p (n t)"),
+            )
+
+        def gather_x(i):
+            lo, hi = 2 * i * PASS, 2 * (i + 1) * PASS
+            xg = work.tile([P, hi - lo, XB], BF16, name="xg", align_bytes=64)
+            nc.vector.tensor_copy(
+                xg[:].rearrange("p s h -> p (s h)").bitcast(U32),
+                xp[:].rearrange("p t h -> p (t h)").bitcast(U32).indirect(offsets[:, lo // 16 : hi // 16]),
+            )
+            for u in range(2):
+                bank = psum.tile([P, XB, PACK, P], BF16, name="bank")
+                quads = xg[:, u * PASS : (u + 1) * PASS, :].rearrange("p (q t) h -> p q t h", t=PACK)
+                for h in range(XB):
+                    for t in range(PACK):
+                        nc.tensor.transpose(bank[:, h, t, :], quads[:, :, t, h], ident_b[:])
+                nc.scalar.copy(
+                    x_turned[i][:, u, :, :].rearrange("p (h k) t -> p h k t", h=XB), bank[:].rearrange("p h t k -> p h k t")
+                )
+
+        def quantize_x(i):
+            nc.vector.quantize_mx(
+                out=x_codes[i][:].rearrange("p u k -> p (u k)").bitcast(E4M3X4),
+                scales=x_scales[i][:].rearrange("p u k -> p (u k)"),
+                in_=x_turned[i][:].rearrange("p u k t -> p (u k t)"),
+            )
+
+        accs = [[acc_pool.tile([P, N], F32, name="acc") for h in range(XB)] for e in range(E)]
+
+        def multiply(c):
+            e, u = divmod(c, 2)
+            for h in range(XB):
+                cols = slice(h * P, (h + 1) * P)
+                nc.tensor.matmul_mx(
+                    out=accs[e][h][:],
+                    lhsT=x_codes[e][:, u, cols].bitcast(E4M3X4),
+                    lhsT_scale=x_scales[e][:, u, cols],
+                    rhs=g_codes[c][:].bitcast(E5M2X4),
+                    rhs_scale=g_scales[c][:],
+                    start=(u == 0),
+                    stop=(u == 1),
+                )
+
+        def store(e, h, engine_copy, queue):
+            res = work.tile([P, N], F32, name="res")
+            engine_copy(res[:], accs[e][h][:])
+            queue.dma_start(out[e, h * P : (h + 1) * P, :], res[:])
+
+        gather_g(0, 0, 1024)
+        gather_g(0, 1024, 2048)
+        gather_g(1, 0, 1024)
+        gather_g(1, 1024, 2048)
+        for i in range(T // X_CHUNK):
+            nc.scalar.copy(xp[:, i * X_CHUNK : (i + 1) * X_CHUNK, :], x_raw[i][:].rearrange("p h t -> p t h"))
+        gather_g(2, 0, 1024)
+        gather_g(2, 1024, 2048)
+        gather_x(0)
+        gather_x(1)
+        gather_g(3, 0, 512)
+        quantize_x(0)
+        gather_g(3, 512, 1024)
+        quantize_x(1)
+        quantize_g(0, 0, 4)
+        multiply(0)
+        gather_g(3, 1024, 1536)
+        quantize_g(1, 0, 4)
+        multiply(1)
+        gather_g(3, 1536, 2048)
+        store(0, 0, nc.scalar.copy, nc.sync)
+        store(0, 1, nc.scalar.copy, nc.sync)
+        quantize_g(2, 0, 4)
+        quantize_g(3, 0, 2)
+        quantize_g(3, 2, 3)
+        multiply(2)
+        quantize_g(3, 3, 4)
+        multiply(3)
+        store(1, 0, nc.scalar.copy, nc.sync)
+        store(1, 1, nc.vector.tensor_copy, nc.scalar)

@@ -31,22 +31,23 @@ def tile_moe_bdw_lin_none_kernel(tc, xT, dyT, gate, offs, out):
     nc = tc.nc
     with ExitStack() as ctx:
         keep = ctx.enter_context(tc.tile_pool(name="keep", bufs=1))
-        work = ctx.enter_context(tc.tile_pool(name="work", bufs=3))
+        work = ctx.enter_context(tc.tile_pool(name="work", bufs=4))
         psum = ctx.enter_context(tc.psum_pool(name="psum", bufs=4))
         acc_pool = ctx.enter_context(tc.psum_pool(name="acc_pool", bufs=4))
 
         offsets = keep.tile([P, S // 16], U16, name="offsets")
         nc.sync.dma_start(offsets[:], offs)
         gate_rows = keep.tile([P, P], F32, name="gate_rows")
-        nc.sync.dma_start(gate_rows[:], gate[0 : P * P // S, :].rearrange("r (c p) -> (r c) p", p=P))
+        nc.scalar.dma_start(gate_rows[:], gate[0 : P * P // S, :].rearrange("r (c p) -> (r c) p", p=P))
 
         dy = [keep.tile([P, T], F32, name=f"dy{b}") for b in range(GB)]
         x_raw = [keep.tile([P, XB, X_CHUNK], F32, name=f"xraw{i}") for i in range(T // X_CHUNK)]
-        for b in range(GB - 1):
+        for b in range(2):
             nc.sync.dma_start(dy[b][:], dyT[b * P : (b + 1) * P, :])
         for i in range(T // X_CHUNK):
             nc.sync.dma_start(x_raw[i][:], xT[:, i * X_CHUNK : (i + 1) * X_CHUNK].rearrange("(h p) t -> p h t", p=P))
-        nc.sync.dma_start(dy[GB - 1][:], dyT[(GB - 1) * P : GB * P, :])
+        for b in range(2, GB):
+            nc.sync.dma_start(dy[b][:], dyT[b * P : (b + 1) * P, :])
 
         ident_f = keep.tile([P, P], F32, name="ident_f")
         make_identity(nc, ident_f[:])
@@ -56,40 +57,46 @@ def tile_moe_bdw_lin_none_kernel(tc, xT, dyT, gate, offs, out):
         gate_bank = psum.tile([P, P], F32, name="bank")
         nc.tensor.transpose(gate_bank[:], gate_rows[:], ident_f[:])
         gate_cols = keep.tile([P, S // P], F32, name="gate_cols")
-        nc.scalar.copy(gate_cols[:], gate_bank[:, 0 : S // P])
+        nc.vector.tensor_copy(gate_cols[:], gate_bank[:, 0 : S // P])
         gates = keep.tile([P, S], F32, name="gates")
         for c in range(PASSES):
             bank = psum.tile([P, PACK, P], F32, name="bank")
             for t in range(PACK):
                 col = PACK * c + t
                 nc.tensor.transpose(bank[:, t, :], gate_cols[:, col : col + 1].to_broadcast([P, P]), ident_f[:])
-            nc.scalar.copy(gates[:, c * PASS : (c + 1) * PASS], bank[:].rearrange("p t n -> p (t n)"))
+            copy_out = nc.scalar.copy if c % 2 else nc.vector.tensor_copy
+            copy_out(gates[:, c * PASS : (c + 1) * PASS], bank[:].rearrange("p t n -> p (t n)"))
 
         xp = keep.tile([P, T, XB], BF16, name="xp", align_bytes=64)
 
-        g_turned = [keep.tile([P, N, PACK], BF16, name=f"gt{c}", align_bytes=64) for c in range(PASSES)]
-        g_codes = [keep.tile([P, N], U32, name=f"gc{c}", align_bytes=64) for c in range(PASSES)]
-        g_scales = [keep.tile([P, N], U8, name=f"gs{c}", align_bytes=64) for c in range(PASSES)]
+        g_turned = keep.tile([P, PASSES * N, PACK], BF16, name="g_turned", align_bytes=64)
+        g_codes = keep.tile([P, PASSES * N], U32, name="g_codes", align_bytes=64)
+        g_scales = keep.tile([P, PASSES * N], U8, name="g_scales", align_bytes=64)
         x_turned = [keep.tile([P, 2, K, PACK], BF16, name=f"xt{i}", align_bytes=64) for i in range(PASSES // 2)]
         x_codes = [keep.tile([P, 2, K], U32, name=f"xc{i}", align_bytes=64) for i in range(PASSES // 2)]
         x_scales = [keep.tile([P, 2, K], U8, name=f"xs{i}", align_bytes=64) for i in range(PASSES // 2)]
 
+        g_tiles = {}
+
         def gather_g(b, lo, hi):
-            g = work.tile([P, hi - lo], F32, name=f"g{hi - lo}")
+            g = keep.tile([P, hi - lo], F32, name=f"g{b}_{lo}")
             nc.vector.tensor_tensor(g[:], dy[b][:].indirect(offsets[:, lo // 16 : hi // 16]), gates[:, lo:hi], MULT)
             for c in range(lo // PASS, hi // PASS):
-                bank = psum.tile([P, PACK, P], F32, name="bank")
-                quads = g[:, c * PASS - lo : (c + 1) * PASS - lo].rearrange("p (q t) -> p q t", t=PACK)
-                for t in range(PACK):
-                    nc.tensor.transpose(bank[:, t, :], quads[:, :, t], ident_f[:])
-                nc.scalar.copy(g_turned[c][:, b * P : (b + 1) * P, :], bank[:].rearrange("p t n -> p n t"))
+                g_tiles[b, c] = g[:, c * PASS - lo : (c + 1) * PASS - lo]
 
-        def quantize_g(c, b0, b1):
-            cols = slice(b0 * P, b1 * P)
+        def turn_g(b, c):
+            bank = psum.tile([P, PACK, P], F32, name="bank")
+            quads = g_tiles[b, c].rearrange("p (q t) -> p q t", t=PACK)
+            for t in range(PACK):
+                nc.tensor.transpose(bank[:, t, :], quads[:, :, t], ident_f[:])
+            nc.scalar.copy(g_turned[:, c * N + b * P : c * N + (b + 1) * P, :], bank[:].rearrange("p t n -> p n t"))
+
+        def quantize_g(lo, hi):
+            cols = slice(lo, hi)
             nc.vector.quantize_mx(
-                out=g_codes[c][:, cols].bitcast(E5M2X4),
-                scales=g_scales[c][:, cols],
-                in_=g_turned[c][:, cols, :].rearrange("p n t -> p (n t)"),
+                out=g_codes[:, cols].bitcast(E5M2X4),
+                scales=g_scales[:, cols],
+                in_=g_turned[:, cols, :].rearrange("p n t -> p (n t)"),
             )
 
         def gather_x(i):
@@ -126,8 +133,8 @@ def tile_moe_bdw_lin_none_kernel(tc, xT, dyT, gate, offs, out):
                     out=accs[e][h][:],
                     lhsT=x_codes[e][:, u, cols].bitcast(E4M3X4),
                     lhsT_scale=x_scales[e][:, u, cols],
-                    rhs=g_codes[c][:].bitcast(E5M2X4),
-                    rhs_scale=g_scales[c][:],
+                    rhs=g_codes[:, c * N : (c + 1) * N].bitcast(E5M2X4),
+                    rhs_scale=g_scales[:, c * N : (c + 1) * N],
                     start=(u == 0),
                     stop=(u == 1),
                 )
@@ -137,33 +144,46 @@ def tile_moe_bdw_lin_none_kernel(tc, xT, dyT, gate, offs, out):
             engine_copy(res[:], accs[e][h][:])
             queue.dma_start(out[e, h * P : (h + 1) * P, :], res[:])
 
-        gather_g(0, 0, 1024)
+        gather_g(0, 0, 512)
+        turn_g(0, 0)
+        gather_g(0, 512, 1024)
+        turn_g(0, 1)
         gather_g(0, 1024, 2048)
-        gather_g(1, 0, 1024)
-        gather_g(1, 1024, 2048)
         for i in range(T // X_CHUNK):
             nc.scalar.copy(xp[:, i * X_CHUNK : (i + 1) * X_CHUNK, :], x_raw[i][:].rearrange("p h t -> p t h"))
-        gather_g(2, 0, 1024)
-        gather_g(2, 1024, 2048)
+        turn_g(0, 2)
+        turn_g(0, 3)
+        gather_g(1, 0, 1024)
+        gather_g(1, 1024, 2048)
+        for c in range(PASSES):
+            turn_g(1, c)
         gather_x(0)
         gather_x(1)
+        gather_g(2, 0, 1024)
+        gather_g(2, 1024, 2048)
+        for c in range(PASSES):
+            turn_g(2, c)
         gather_g(3, 0, 512)
+        turn_g(3, 0)
         quantize_x(0)
-        gather_g(3, 512, 1024)
         quantize_x(1)
-        quantize_g(0, 0, 4)
+        gather_g(3, 512, 1024)
+        turn_g(3, 1)
+        quantize_g(0, N)
         multiply(0)
         gather_g(3, 1024, 1536)
-        quantize_g(1, 0, 4)
+        turn_g(3, 2)
+        quantize_g(N, 2 * N)
         multiply(1)
-        gather_g(3, 1536, 2048)
         store(0, 0, nc.scalar.copy, nc.sync)
-        store(0, 1, nc.scalar.copy, nc.sync)
-        quantize_g(2, 0, 4)
-        quantize_g(3, 0, 2)
-        quantize_g(3, 2, 3)
+        gather_g(3, 1536, 2048)
+        turn_g(3, 3)
+        quantize_g(2 * N, 3 * N)
         multiply(2)
-        quantize_g(3, 3, 4)
+        quantize_g(3 * N, 3 * N + 2 * P)
+        quantize_g(3 * N + 2 * P, 3 * N + 3 * P)
+        store(0, 1, nc.vector.tensor_copy, nc.sync)
+        quantize_g(3 * N + 3 * P, 4 * N)
         multiply(3)
         store(1, 0, nc.scalar.copy, nc.sync)
         store(1, 1, nc.vector.tensor_copy, nc.scalar)

@@ -42,12 +42,11 @@ def tile_moe_bdw_lin_none_kernel(tc, xT, dyT, gate, offs, out):
 
         dy = [keep.tile([P, T], F32, name=f"dy{b}") for b in range(GB)]
         x_raw = [keep.tile([P, XB, X_CHUNK], F32, name=f"xraw{i}") for i in range(T // X_CHUNK)]
-        for b in range(2):
+        for b in range(GB - 1):
             nc.sync.dma_start(dy[b][:], dyT[b * P : (b + 1) * P, :])
         for i in range(T // X_CHUNK):
             nc.sync.dma_start(x_raw[i][:], xT[:, i * X_CHUNK : (i + 1) * X_CHUNK].rearrange("(h p) t -> p h t", p=P))
-        for b in range(2, GB):
-            nc.sync.dma_start(dy[b][:], dyT[b * P : (b + 1) * P, :])
+        nc.sync.dma_start(dy[GB - 1][:], dyT[(GB - 1) * P : GB * P, :])
 
         ident_f = keep.tile([P, P], F32, name="ident_f")
         make_identity(nc, ident_f[:])
@@ -67,19 +66,17 @@ def tile_moe_bdw_lin_none_kernel(tc, xT, dyT, gate, offs, out):
             copy_out = nc.scalar.copy if c % 2 else nc.vector.tensor_copy
             copy_out(gates[:, c * PASS : (c + 1) * PASS], bank[:].rearrange("p t n -> p (t n)"))
 
-        xp = keep.tile([P, T, XB], BF16, name="xp", align_bytes=64)
-
-        g_turned = keep.tile([P, PASSES * N, PACK], BF16, name="g_turned", align_bytes=64)
+        g_turned = [keep.tile([P, N, PACK], BF16, name=f"g_turned{c}", tag=f"turned{c}", align_bytes=64) for c in range(PASSES)]
         g_codes = keep.tile([P, PASSES * N], U32, name="g_codes", align_bytes=64)
         g_scales = keep.tile([P, PASSES * N], U8, name="g_scales", align_bytes=64)
-        x_turned = [keep.tile([P, 2, K, PACK], BF16, name=f"xt{i}", align_bytes=64) for i in range(PASSES // 2)]
+        x_turned = [keep.tile([P, 2, K, PACK], BF16, name=f"xt{i}", tag=f"xturned{i}", align_bytes=64) for i in range(PASSES // 2)]
         x_codes = [keep.tile([P, 2, K], U32, name=f"xc{i}", align_bytes=64) for i in range(PASSES // 2)]
         x_scales = [keep.tile([P, 2, K], U8, name=f"xs{i}", align_bytes=64) for i in range(PASSES // 2)]
 
-        g_tiles = {}
+        g_tiles, x_tiles = {}, {}
 
-        def gather_g(b, lo, hi):
-            g = keep.tile([P, hi - lo], F32, name=f"g{b}_{lo}")
+        def gather_g(b, lo, hi, tag=None):
+            g = keep.tile([P, hi - lo], F32, name=f"g{b}_{lo}", tag=tag or f"g{b}_{lo}", align_bytes=64)
             nc.vector.tensor_tensor(g[:], dy[b][:].indirect(offsets[:, lo // 16 : hi // 16]), gates[:, lo:hi], MULT)
             for c in range(lo // PASS, hi // PASS):
                 g_tiles[b, c] = g[:, c * PASS - lo : (c + 1) * PASS - lo]
@@ -89,14 +86,14 @@ def tile_moe_bdw_lin_none_kernel(tc, xT, dyT, gate, offs, out):
             quads = g_tiles[b, c].rearrange("p (q t) -> p q t", t=PACK)
             for t in range(PACK):
                 nc.tensor.transpose(bank[:, t, :], quads[:, :, t], ident_f[:])
-            nc.scalar.copy(g_turned[:, c * N + b * P : c * N + (b + 1) * P, :], bank[:].rearrange("p t n -> p n t"))
+            nc.scalar.copy(g_turned[c][:, b * P : (b + 1) * P, :], bank[:].rearrange("p t n -> p n t"))
 
-        def quantize_g(lo, hi):
-            cols = slice(lo, hi)
+        def quantize_g(c, lo, hi):
+            cols = slice(c * N + lo * P, c * N + hi * P)
             nc.vector.quantize_mx(
                 out=g_codes[:, cols].bitcast(E5M2X4),
                 scales=g_scales[:, cols],
-                in_=g_turned[:, cols, :].rearrange("p n t -> p (n t)"),
+                in_=g_turned[c][:, lo * P : hi * P, :].rearrange("p n t -> p (n t)"),
             )
 
         def gather_x(i):
@@ -106,6 +103,10 @@ def tile_moe_bdw_lin_none_kernel(tc, xT, dyT, gate, offs, out):
                 xg[:].rearrange("p s h -> p (s h)").bitcast(U32),
                 xp[:].rearrange("p t h -> p (t h)").bitcast(U32).indirect(offsets[:, lo // 16 : hi // 16]),
             )
+            x_tiles[i] = xg
+
+        def turn_x(i):
+            xg = x_tiles[i]
             for u in range(2):
                 bank = psum.tile([P, XB, PACK, P], BF16, name="bank")
                 quads = xg[:, u * PASS : (u + 1) * PASS, :].rearrange("p (q t) h -> p q t h", t=PACK)
@@ -148,42 +149,45 @@ def tile_moe_bdw_lin_none_kernel(tc, xT, dyT, gate, offs, out):
         turn_g(0, 0)
         gather_g(0, 512, 1024)
         turn_g(0, 1)
-        gather_g(0, 1024, 2048)
-        for i in range(T // X_CHUNK):
-            nc.scalar.copy(xp[:, i * X_CHUNK : (i + 1) * X_CHUNK, :], x_raw[i][:].rearrange("p h t -> p t h"))
+        gather_g(0, 1024, 2048, tag="first")
         turn_g(0, 2)
         turn_g(0, 3)
-        gather_g(1, 0, 1024)
-        gather_g(1, 1024, 2048)
+        xp = keep.tile([P, T, XB], BF16, name="xp", tag="first", align_bytes=64)
+        for i in range(T // X_CHUNK):
+            nc.scalar.copy(xp[:, i * X_CHUNK : (i + 1) * X_CHUNK, :], x_raw[i][:].rearrange("p h t -> p t h"))
+        gather_g(1, 0, 2048)
         for c in range(PASSES):
             turn_g(1, c)
+        gather_g(2, 0, 2048)
+        turn_g(2, 0)
+        turn_g(2, 1)
         gather_x(0)
+        turn_x(0)
         gather_x(1)
-        gather_g(2, 0, 1024)
-        gather_g(2, 1024, 2048)
-        for c in range(PASSES):
-            turn_g(2, c)
-        gather_g(3, 0, 512)
+        turn_x(1)
+        turn_g(2, 2)
+        turn_g(2, 3)
+        gather_g(3, 0, 512, tag="first")
         turn_g(3, 0)
         quantize_x(0)
-        quantize_x(1)
-        gather_g(3, 512, 1024)
+        gather_g(3, 512, 1024, tag="xturned0")
         turn_g(3, 1)
-        quantize_g(0, N)
+        quantize_x(1)
+        quantize_g(0, 0, 4)
         multiply(0)
-        gather_g(3, 1024, 1536)
+        gather_g(3, 1024, 1536, tag="turned0")
         turn_g(3, 2)
-        quantize_g(N, 2 * N)
+        quantize_g(1, 0, 4)
         multiply(1)
+        gather_g(3, 1536, 2048, tag="turned1")
         store(0, 0, nc.scalar.copy, nc.sync)
-        gather_g(3, 1536, 2048)
         turn_g(3, 3)
-        quantize_g(2 * N, 3 * N)
+        quantize_g(2, 0, 4)
         multiply(2)
-        quantize_g(3 * N, 3 * N + 2 * P)
-        quantize_g(3 * N + 2 * P, 3 * N + 3 * P)
+        quantize_g(3, 0, 2)
+        quantize_g(3, 2, 3)
         store(0, 1, nc.vector.tensor_copy, nc.sync)
-        quantize_g(3 * N + 3 * P, 4 * N)
+        quantize_g(3, 3, 4)
         multiply(3)
         store(1, 0, nc.scalar.copy, nc.sync)
         store(1, 1, nc.vector.tensor_copy, nc.scalar)

@@ -24,7 +24,7 @@ PASS = P * PACK
 PASSES = S // PASS
 XB = K // P
 GB = N // P
-X_CHUNK = 640
+X_CUTS = ((0, 640), (640, 1280), (1280, 1920), (1920, 2560))
 
 
 def tile_moe_bdw_lin_none_kernel(tc, xT, dyT, gate, offs, out):
@@ -41,17 +41,15 @@ def tile_moe_bdw_lin_none_kernel(tc, xT, dyT, gate, offs, out):
         nc.scalar.dma_start(gate_rows[:], gate[0 : P * P // S, :].rearrange("r (c p) -> (r c) p", p=P))
 
         dy = [keep.tile([P, T], F32, name=f"dy{b}") for b in range(GB)]
-        x_raw = [keep.tile([P, XB, X_CHUNK], F32, name=f"xraw{i}") for i in range(T // X_CHUNK)]
+        x_raw = [keep.tile([P, XB, hi - lo], F32, name=f"xraw{lo}") for lo, hi in X_CUTS]
         for b in range(GB - 1):
             nc.sync.dma_start(dy[b][:], dyT[b * P : (b + 1) * P, :])
-        for i in range(T // X_CHUNK):
-            nc.sync.dma_start(x_raw[i][:], xT[:, i * X_CHUNK : (i + 1) * X_CHUNK].rearrange("(h p) t -> p h t", p=P))
+        for raw, (lo, hi) in zip(x_raw, X_CUTS):
+            nc.sync.dma_start(raw[:], xT[:, lo:hi].rearrange("(h p) t -> p h t", p=P))
         nc.sync.dma_start(dy[GB - 1][:], dyT[(GB - 1) * P : GB * P, :])
 
         ident_f = keep.tile([P, P], F32, name="ident_f")
         make_identity(nc, ident_f[:])
-        ident_b = keep.tile([P, P], BF16, name="ident_b")
-        make_identity(nc, ident_b[:])
 
         gate_bank = psum.tile([P, P], F32, name="bank")
         nc.tensor.transpose(gate_bank[:], gate_rows[:], ident_f[:])
@@ -88,6 +86,20 @@ def tile_moe_bdw_lin_none_kernel(tc, xT, dyT, gate, offs, out):
                 nc.tensor.transpose(bank[:, t, :], quads[:, :, t], ident_f[:])
             nc.scalar.copy(g_turned[c][:, b * P : (b + 1) * P, :], bank[:].rearrange("p t n -> p n t"))
 
+        pairs = {}
+
+        def round_g(b, c, copy):
+            pairs[b, c] = keep.tile([P, PASS], BF16, name=f"gb{b}_{c}", align_bytes=64)
+            copy(pairs[b, c][:], g_tiles[b, c])
+
+        def turn_pairs(b, c):
+            bank = psum.tile([P, 2, P], F32, name="bank")
+            words = pairs[b, c][:].bitcast(F32).rearrange("p (q u) -> p q u", u=2)
+            for u in range(2):
+                nc.tensor.transpose(bank[:, u, :], words[:, :, u], ident_f[:])
+            turned = g_turned[c][:, b * P : (b + 1) * P, :].rearrange("p n t -> p (n t)").bitcast(F32)
+            nc.scalar.copy(turned.rearrange("p (n u) -> p n u", u=2), bank[:].rearrange("p u n -> p n u"))
+
         def quantize_g(c, lo, hi):
             cols = slice(c * N + lo * P, c * N + hi * P)
             nc.vector.quantize_mx(
@@ -108,13 +120,15 @@ def tile_moe_bdw_lin_none_kernel(tc, xT, dyT, gate, offs, out):
         def turn_x(i):
             xg = x_tiles[i]
             for u in range(2):
-                bank = psum.tile([P, XB, PACK, P], BF16, name="bank")
-                quads = xg[:, u * PASS : (u + 1) * PASS, :].rearrange("p (q t) h -> p q t h", t=PACK)
-                for h in range(XB):
-                    for t in range(PACK):
-                        nc.tensor.transpose(bank[:, h, t, :], quads[:, :, t, h], ident_b[:])
+                bank = psum.tile([P, PACK, P], F32, name="bank")
+                words = xg[:, u * PASS : (u + 1) * PASS, :].rearrange("p s h -> p (s h)").bitcast(F32)
+                quads = words.rearrange("p (q t) -> p q t", t=PACK)
+                for t in range(PACK):
+                    nc.tensor.transpose(bank[:, t, :], quads[:, :, t], ident_f[:])
+                halves = bank[:].rearrange("p t k -> p (t k)").bitcast(BF16)
                 nc.scalar.copy(
-                    x_turned[i][:, u, :, :].rearrange("p (h k) t -> p h k t", h=XB), bank[:].rearrange("p h t k -> p h k t")
+                    x_turned[i][:, u, :, :].rearrange("p (h k) t -> p h k t", h=XB),
+                    halves.rearrange("p (t k h) -> p h k t", t=PACK, h=XB),
                 )
 
         def quantize_x(i):
@@ -145,16 +159,15 @@ def tile_moe_bdw_lin_none_kernel(tc, xT, dyT, gate, offs, out):
             engine_copy(res[:], accs[e][h][:])
             queue.dma_start(out[e, h * P : (h + 1) * P, :], res[:])
 
-        gather_g(0, 0, 512)
-        turn_g(0, 0)
-        gather_g(0, 512, 1024)
-        turn_g(0, 1)
-        gather_g(0, 1024, 2048, tag="first")
-        turn_g(0, 2)
-        turn_g(0, 3)
+        for lo, hi, tag in ((0, 512, None), (512, 1024, None), (1024, 2048, "first")):
+            gather_g(0, lo, hi, tag=tag)
+            for c in range(lo // PASS, hi // PASS):
+                round_g(0, c, nc.scalar.copy)
+            for c in range(lo // PASS, hi // PASS):
+                turn_pairs(0, c)
         xp = keep.tile([P, T, XB], BF16, name="xp", tag="first", align_bytes=64)
-        for i in range(T // X_CHUNK):
-            nc.scalar.copy(xp[:, i * X_CHUNK : (i + 1) * X_CHUNK, :], x_raw[i][:].rearrange("p h t -> p t h"))
+        for raw, (lo, hi) in zip(x_raw, X_CUTS):
+            nc.scalar.copy(xp[:, lo:hi, :], raw[:].rearrange("p h t -> p t h"))
         gather_g(1, 0, 2048)
         for c in range(PASSES):
             turn_g(1, c)
@@ -180,8 +193,9 @@ def tile_moe_bdw_lin_none_kernel(tc, xT, dyT, gate, offs, out):
         quantize_g(1, 0, 4)
         multiply(1)
         gather_g(3, 1536, 2048, tag="turned1")
+        round_g(3, 3, nc.vector.tensor_copy)
         store(0, 0, nc.scalar.copy, nc.sync)
-        turn_g(3, 3)
+        turn_pairs(3, 3)
         quantize_g(2, 0, 4)
         multiply(2)
         quantize_g(3, 0, 2)

@@ -174,12 +174,14 @@ def tile_moe_bdw_lin_none_kernel(tc, xT, dyT, gate, offs, out):
         gather_g(2, 0, 2048)
         turn_g(2, 0)
         turn_g(2, 1)
+        round_g(2, 2, nc.scalar.copy)
+        round_g(2, 3, nc.scalar.copy)
         gather_x(0)
         turn_x(0)
+        turn_pairs(2, 2)
+        turn_pairs(2, 3)
         gather_x(1)
         turn_x(1)
-        turn_g(2, 2)
-        turn_g(2, 3)
         gather_g(3, 0, 512, tag="first")
         turn_g(3, 0)
         quantize_x(0)

from contextlib import ExitStack

import concourse.mybir as mybir
from concourse.masks import make_identity

K, T, E, C, N = 256, 2560, 2, 1024, 512
S = E * C

FLOPS = 2 * S * K * N
BYTES = 4 * (K * T + N * T + S + E * K * N) + 2 * S

F32 = mybir.dt.float32
BF16 = mybir.dt.bfloat16
U32 = mybir.dt.uint32
U16 = mybir.dt.uint16
U8 = mybir.dt.uint8
E4M3X4 = mybir.dt.float8_e4m3fn_x4
E5M2X4 = mybir.dt.float8_e5m2_x4
MULT = mybir.AluOpType.mult

P = 128
PACK = 4
PASS = P * PACK
PASSES = S // PASS
XB = K // P
GB = N // P
X_CUTS = ((0, 640), (640, 1280), (1280, 1920), (1920, 2560))


def tile_moe_bdw_lin_none_kernel(tc, xT, dyT, gate, offs, out):
    nc = tc.nc
    with ExitStack() as ctx:
        keep = ctx.enter_context(tc.tile_pool(name="keep", bufs=1))
        work = ctx.enter_context(tc.tile_pool(name="work", bufs=4))
        psum = ctx.enter_context(tc.psum_pool(name="psum", bufs=4))
        acc_pool = ctx.enter_context(tc.psum_pool(name="acc_pool", bufs=4))

        offsets = keep.tile([P, S // 16], U16, name="offsets")
        nc.sync.dma_start(offsets[:], offs)
        gate_rows = keep.tile([P, P], F32, name="gate_rows")
        nc.scalar.dma_start(gate_rows[:], gate[0 : P * P // S, :].rearrange("r (c p) -> (r c) p", p=P))

        dy = [keep.tile([P, T], F32, name=f"dy{b}") for b in range(GB)]
        x_raw = [keep.tile([P, XB, hi - lo], F32, name=f"xraw{lo}") for lo, hi in X_CUTS]
        for b in range(GB - 1):
            nc.sync.dma_start(dy[b][:], dyT[b * P : (b + 1) * P, :])
        for raw, (lo, hi) in zip(x_raw, X_CUTS):
            nc.sync.dma_start(raw[:], xT[:, lo:hi].rearrange("(h p) t -> p h t", p=P))
        nc.sync.dma_start(dy[GB - 1][:], dyT[(GB - 1) * P : GB * P, :])

        ident_f = keep.tile([P, P], F32, name="ident_f")
        make_identity(nc, ident_f[:])

        gate_bank = psum.tile([P, P], F32, name="bank")
        nc.tensor.transpose(gate_bank[:], gate_rows[:], ident_f[:])
        gate_cols = keep.tile([P, S // P], F32, name="gate_cols")
        nc.vector.tensor_copy(gate_cols[:], gate_bank[:, 0 : S // P])
        gates = keep.tile([P, S], F32, name="gates")
        for c in range(PASSES):
            bank = psum.tile([P, PACK, P], F32, name="bank")
            for t in range(PACK):
                col = PACK * c + t
                nc.tensor.transpose(bank[:, t, :], gate_cols[:, col : col + 1].to_broadcast([P, P]), ident_f[:])
            copy_out = nc.scalar.copy if c % 2 else nc.vector.tensor_copy
            copy_out(gates[:, c * PASS : (c + 1) * PASS], bank[:].rearrange("p t n -> p (t n)"))

        g_turned = [keep.tile([P, N, PACK], BF16, name=f"g_turned{c}", tag=f"turned{c}", align_bytes=64) for c in range(PASSES)]
        g_codes = keep.tile([P, PASSES * N], U32, name="g_codes", align_bytes=64)
        g_scales = keep.tile([P, PASSES * N], U8, name="g_scales", align_bytes=64)
        x_turned = [keep.tile([P, 2, K, PACK], BF16, name=f"xt{i}", tag=f"xturned{i}", align_bytes=64) for i in range(PASSES // 2)]
        x_codes = [keep.tile([P, 2, K], U32, name=f"xc{i}", align_bytes=64) for i in range(PASSES // 2)]
        x_scales = [keep.tile([P, 2, K], U8, name=f"xs{i}", align_bytes=64) for i in range(PASSES // 2)]

        g_tiles, x_tiles = {}, {}

        def gather_g(b, lo, hi, tag=None):
            g = keep.tile([P, hi - lo], F32, name=f"g{b}_{lo}", tag=tag or f"g{b}_{lo}", align_bytes=64)
            nc.vector.tensor_tensor(g[:], dy[b][:].indirect(offsets[:, lo // 16 : hi // 16]), gates[:, lo:hi], MULT)
            for c in range(lo // PASS, hi // PASS):
                g_tiles[b, c] = g[:, c * PASS - lo : (c + 1) * PASS - lo]

        def turn_g(b, c):
            bank = psum.tile([P, PACK, P], F32, name="bank")
            quads = g_tiles[b, c].rearrange("p (q t) -> p q t", t=PACK)
            for t in range(PACK):
                nc.tensor.transpose(bank[:, t, :], quads[:, :, t], ident_f[:])
            nc.scalar.copy(g_turned[c][:, b * P : (b + 1) * P, :], bank[:].rearrange("p t n -> p n t"))

        pairs = {}

        def round_g(b, c, copy):
            pairs[b, c] = keep.tile([P, PASS], BF16, name=f"gb{b}_{c}", align_bytes=64)
            copy(pairs[b, c][:], g_tiles[b, c])

        def turn_pairs(b, c):
            bank = psum.tile([P, 2, P], F32, name="bank")
            words = pairs[b, c][:].bitcast(F32).rearrange("p (q u) -> p q u", u=2)
            for u in range(2):
                nc.tensor.transpose(bank[:, u, :], words[:, :, u], ident_f[:])
            turned = g_turned[c][:, b * P : (b + 1) * P, :].rearrange("p n t -> p (n t)").bitcast(F32)
            nc.scalar.copy(turned.rearrange("p (n u) -> p n u", u=2), bank[:].rearrange("p u n -> p n u"))

        def quantize_g(c, lo, hi):
            cols = slice(c * N + lo * P, c * N + hi * P)
            nc.vector.quantize_mx(
                out=g_codes[:, cols].bitcast(E5M2X4),
                scales=g_scales[:, cols],
                in_=g_turned[c][:, lo * P : hi * P, :].rearrange("p n t -> p (n t)"),
            )

        def gather_x(i):
            lo, hi = 2 * i * PASS, 2 * (i + 1) * PASS
            xg = work.tile([P, hi - lo, XB], BF16, name="xg", align_bytes=64)
            nc.vector.tensor_copy(
                xg[:].rearrange("p s h -> p (s h)").bitcast(U32),
                xp[:].rearrange("p t h -> p (t h)").bitcast(U32).indirect(offsets[:, lo // 16 : hi // 16]),
            )
            x_tiles[i] = xg

        def turn_x(i):
            xg = x_tiles[i]
            for u in range(2):
                bank = psum.tile([P, PACK, P], F32, name="bank")
                words = xg[:, u * PASS : (u + 1) * PASS, :].rearrange("p s h -> p (s h)").bitcast(F32)
                quads = words.rearrange("p (q t) -> p q t", t=PACK)
                for t in range(PACK):
                    nc.tensor.transpose(bank[:, t, :], quads[:, :, t], ident_f[:])
                halves = bank[:].rearrange("p t k -> p (t k)").bitcast(BF16)
                nc.scalar.copy(
                    x_turned[i][:, u, :, :].rearrange("p (h k) t -> p h k t", h=XB),
                    halves.rearrange("p (t k h) -> p h k t", t=PACK, h=XB),
                )

        def quantize_x(i):
            nc.vector.quantize_mx(
                out=x_codes[i][:].rearrange("p u k -> p (u k)").bitcast(E4M3X4),
                scales=x_scales[i][:].rearrange("p u k -> p (u k)"),
                in_=x_turned[i][:].rearrange("p u k t -> p (u k t)"),
            )

        accs = [[acc_pool.tile([P, N], F32, name="acc") for h in range(XB)] for e in range(E)]

        def multiply(c):
            e, u = divmod(c, 2)
            for h in range(XB):
                cols = slice(h * P, (h + 1) * P)
                nc.tensor.matmul_mx(
                    out=accs[e][h][:],
                    lhsT=x_codes[e][:, u, cols].bitcast(E4M3X4),
                    lhsT_scale=x_scales[e][:, u, cols],
                    rhs=g_codes[:, c * N : (c + 1) * N].bitcast(E5M2X4),
                    rhs_scale=g_scales[:, c * N : (c + 1) * N],
                    start=(u == 0),
                    stop=(u == 1),
                )

        def store(e, h, engine_copy, queue):
            res = work.tile([P, N], F32, name="res")
            engine_copy(res[:], accs[e][h][:])
            queue.dma_start(out[e, h * P : (h + 1) * P, :], res[:])

        for lo, hi, tag in ((0, 512, None), (512, 1024, None), (1024, 2048, "first")):
            gather_g(0, lo, hi, tag=tag)
            for c in range(lo // PASS, hi // PASS):
                round_g(0, c, nc.scalar.copy)
            for c in range(lo // PASS, hi // PASS):
                turn_pairs(0, c)
        xp = keep.tile([P, T, XB], BF16, name="xp", tag="first", align_bytes=64)
        for raw, (lo, hi) in zip(x_raw, X_CUTS):
            nc.scalar.copy(xp[:, lo:hi, :], raw[:].rearrange("p h t -> p t h"))
        gather_g(1, 0, 2048)
        for c in range(PASSES):
            turn_g(1, c)
        gather_g(2, 0, 2048)
        turn_g(2, 0)
        turn_g(2, 1)
        round_g(2, 2, nc.scalar.copy)
        round_g(2, 3, nc.scalar.copy)
        gather_x(0)
        turn_x(0)
        turn_pairs(2, 2)
        turn_pairs(2, 3)
        gather_x(1)
        turn_x(1)
        gather_g(3, 0, 512, tag="first")
        turn_g(3, 0)
        quantize_x(0)
        gather_g(3, 512, 1024, tag="xturned0")
        turn_g(3, 1)
        quantize_x(1)
        quantize_g(0, 0, 4)
        multiply(0)
        gather_g(3, 1024, 1536, tag="turned0")
        turn_g(3, 2)
        quantize_g(1, 0, 4)
        multiply(1)
        gather_g(3, 1536, 2048, tag="turned1")
        round_g(3, 3, nc.vector.tensor_copy)
        store(0, 0, nc.scalar.copy, nc.sync)
        turn_pairs(3, 3)
        quantize_g(2, 0, 4)
        multiply(2)
        quantize_g(3, 0, 2)
        quantize_g(3, 2, 3)
        store(0, 1, nc.vector.tensor_copy, nc.sync)
        quantize_g(3, 3, 4)
        multiply(3)
        store(1, 0, nc.scalar.copy, nc.sync)
        store(1, 1, nc.vector.tensor_copy, nc.scalar)
